import numpy as np
import ml_dtypes


def mxq(x, axis, fmt="e4m3"):
    dtype, down = {"e4m3": (ml_dtypes.float8_e4m3fn, 7), "e5m2": (ml_dtypes.float8_e5m2, 14)}[fmt]
    v = np.moveaxis(np.asarray(x, np.float32).astype(ml_dtypes.bfloat16).astype(np.float64), axis, -1)
    blocks = v.reshape(v.shape[:-1] + (-1, 32))
    amax = np.abs(blocks).max(-1, keepdims=True)
    byte = np.maximum(np.where(amax > 0, np.frexp(amax)[1] - 1 + 127, 0) - down, 1)
    scale = np.exp2(byte - 127.0)
    codes = (blocks / scale).astype(np.float32).astype(dtype).astype(np.float64)
    return np.moveaxis((codes * scale).reshape(v.shape), -1, axis)


WIDE = False


def mx_kscale(k):
    if not WIDE:
        return np.ones(k)
    levels = np.array([10, -10, 5, -5, 0])
    if k % 512:
        return np.exp2(np.random.permutation(np.resize(levels, k // 32))).repeat(32)
    a = np.empty((k // 512, 16))
    for p in range(k // 512):
        a[p, :8] = np.random.permutation(np.resize(levels, 8))
        for g in range(8):
            far = levels[np.abs(levels - a[p, g]) >= 10]
            a[p, g + 8] = far[np.random.randint(len(far))]
    return np.exp2(a.ravel()).repeat(32)


def f64(x):
    return np.asarray(x).astype(np.float64)


E2M1 = np.array([0.0, 0.5, 1.0, 1.5, 2.0, 3.0, 4.0, 6.0, -0.0, -0.5, -1.0, -1.5, -2.0, -3.0, -4.0, -6.0])


def pack_weight(w, fmt):
    k, n = w.shape
    w = f64(np.asarray(w, np.float32).astype(ml_dtypes.bfloat16)).reshape(k // 32, 32, n)
    amax = np.abs(w).max(1)
    if fmt == "e4m3":
        byte = np.frexp(amax)[1] - 1 + 127 - 7
    else:
        mant, ex = np.frexp(amax / 6.0)
        byte = np.where(mant > 0.5, ex, ex - 1) + 127
    byte = np.clip(np.where(amax > 0, byte, 1), 1, 254)
    scaled = (w * np.exp2(127.0 - byte)[:, None, :]).reshape(k, n).astype(np.float32)
    by_word = np.ascontiguousarray(scaled.reshape(k // 512, 128, 4, n).transpose(0, 1, 3, 2))
    if fmt == "e4m3":
        words = by_word.astype(ml_dtypes.float8_e4m3fn).view(np.uint8)
    else:
        c = by_word.astype(ml_dtypes.float4_e2m1fn).view(np.uint8) & 0xF
        words = (c[..., 0::2] | (c[..., 1::2] << 4)).reshape(k // 512, 128, 2 * n)
    return np.ascontiguousarray(words), np.ascontiguousarray(byte.astype(np.uint8).reshape(k // 512, 16, n))


def unpack_weight(words, scales, fmt):
    g, _, n = scales.shape
    words = np.ascontiguousarray(words).reshape(g, 128, n, -1)
    if fmt == "e4m3":
        vals = words.view(ml_dtypes.float8_e4m3fn).astype(np.float64)
    else:
        nib = np.empty((g, 128, n, 4), np.uint8)
        nib[..., 0::2] = words & 0xF
        nib[..., 1::2] = words >> 4
        vals = E2M1[nib]
    vals = vals * np.repeat(np.exp2(scales.astype(np.float64) - 127.0), 8, axis=1)[..., None]
    return vals.transpose(0, 1, 3, 2).reshape(g * 512, n)


def gelu(v):
    return 0.5 * v * (1.0 + np.tanh(np.sqrt(2.0 / np.pi) * (v + 0.044715 * v**3)))


O, K, M, T = 1024, 2048, 512, 1536


def setup_inputs():
    n = np.random.standard_normal
    s = mx_kscale(K)[:, None]
    x = n((K, T)); x[:O] *= 6.0
    w = n((K, M)) / np.sqrt(K) / s; w[:O] /= 2.0
    p_x4 = pack_weight(x[O:] * s[O:], "e2m1")
    p_w4 = pack_weight(w[O:], "e2m1")
    return {
        "x8": (x[:O] * s[:O]).astype(np.float32),
        "w8": (w[:O]).astype(np.float32),
        "x4_words": p_x4[0],
        "x4_scales": p_x4[1],
        "w4_words": p_w4[0],
        "w4_scales": p_w4[1],
        "b": (0.3 * n(512)).astype(np.float32),
    }


def reference(x8, w8, x4_words, x4_scales, w4_words, w4_scales, b):
    x8_ = mxq(f64(x8), 0, "e4m3")
    w8_ = mxq(f64(w8), 0, "e4m3")
    x4_ = unpack_weight(x4_words, x4_scales, "e2m1")
    w4_ = unpack_weight(w4_words, w4_scales, "e2m1")
    y = w8_.T @ x8_ + w4_.T @ x4_
    return gelu(y + f64(b)[:, None])

@@ -1,0 +1,209 @@
+from contextlib import ExitStack
+
+import concourse.mybir as mybir
+from concourse.masks import make_identity
+
+K, N, T = 1024, 512, 1536
+
+F32 = mybir.dt.float32
+BF16 = mybir.dt.bfloat16
+I32 = mybir.dt.int32
+U32 = mybir.dt.uint32
+U8 = mybir.dt.uint8
+E4M3X4 = mybir.dt.float8_e4m3fn_x4
+E2M1X4 = mybir.dt.float4_e2m1fn_x4
+GELU = mybir.ActivationFunctionType.Gelu_apprx_tanh
+
+P = 128
+PASSES = 2
+M_TILES = N // P
+T_TILE = 512
+PIECE = 256
+
+FLOPS = 2 * N * (2 * K) * T
+
+
+def tile_mix_atom_fm_gelu_kernel(tc, x8, w8, x4_words, x4_scales, w4_words, w4_scales, b, out):
+    nc = tc.nc
+    with ExitStack() as ctx:
+        keep = ctx.enter_context(tc.tile_pool(name="keep", bufs=1))
+        results = ctx.enter_context(tc.tile_pool(name="results", bufs=12))
+        psum = ctx.enter_context(tc.psum_pool(name="psum", bufs=1))
+        ctx.enter_context(tc.manual_schedule())
+
+        w8_raw = [keep.tile([P, 4, N], F32, name="w8_raw%d" % a, align_bytes=64) for a in range(PASSES)]
+        w8_grp = [keep.tile([P, N, 4], BF16, name="w8_grp%d" % a, align_bytes=64) for a in range(PASSES)]
+        w8_code = [keep.tile([P, N], U32, name="w8_code%d" % a, align_bytes=64) for a in range(PASSES)]
+        w8_scale = [keep.tile([P, N], U8, name="w8_scale%d" % a, align_bytes=64) for a in range(PASSES)]
+        loads = [(0, 0, 768), (0, 768, 1536), (1, 0, 512), (1, 512, 1024), (1, 1024, 1536)]
+        x8_raw = [keep.tile([P, 4, t1 - t0], F32, name="x8_raw%d_%d" % (a, t0), align_bytes=64) for a, t0, t1 in loads]
+        x8_grp = [keep.tile([P, T, 4], BF16, name="x8_grp%d" % a, align_bytes=64) for a in range(PASSES)]
+        x8_code = [keep.tile([P, T], U32, name="x8_code%d" % a, align_bytes=64) for a in range(PASSES)]
+        x8_scale = [keep.tile([P, T], U8, name="x8_scale%d" % a, align_bytes=64) for a in range(PASSES)]
+        w4_word = keep.tile([P, PASSES, 2 * N], U8, name="w4_word", align_bytes=64)
+        x4_word = keep.tile([P, PASSES, 2 * T], U8, name="x4_word", align_bytes=64)
+        w4_scale = keep.tile([P, PASSES, N], U8, name="w4_scale", align_bytes=64)
+        x4_scale = keep.tile([P, PASSES, T], U8, name="x4_scale", align_bytes=64)
+        ident = keep.tile([P, P], F32, name="ident", align_bytes=64)
+        bias_rows = keep.tile([P, P], F32, name="bias_rows", align_bytes=64)
+        bias = keep.tile([P, M_TILES], F32, name="bias", align_bytes=64)
+        warm = keep.tile([P, 1], F32, name="warm", align_bytes=64)
+
+        def load_w8(a):
+            nc.sync.dma_start(out=w8_raw[a][:], in_=w8[512 * a : 512 * (a + 1), :].rearrange("(p j) n -> p j n", j=4))
+
+        def load_x8(i):
+            a, t0, t1 = loads[i]
+            nc.sync.dma_start(out=x8_raw[i][:], in_=x8[512 * a : 512 * (a + 1), t0:t1].rearrange("(p j) t -> p j t", j=4))
+
+        load_w8(0)
+        nc.sync.dma_start(out=w4_word[:].bitcast(I32), in_=w4_words.bitcast(I32).rearrange("a p w -> p a w"))
+        nc.sync.dma_start(out=x4_word[:].bitcast(I32), in_=x4_words.bitcast(I32).rearrange("a p w -> p a w"))
+
+        nc.vector.memset(x4_scale[:].bitcast(I32), 0)
+        nc.vector.memset(bias_rows[:], 0.0)
+        nc.vector.memset(w4_scale[:].bitcast(I32), 0)
+        nc.vector.memset(warm[:], 0.0)
+
+        def load_scales(engine, plane, source):
+            rows = source.bitcast(I32).rearrange("a (q r) c -> r q a c", r=4)
+            for r in range(4):
+                engine.dma_start(out=plane[:].bitcast(I32)[r:P:32], in_=rows[r])
+
+        load_scales(nc.scalar, x4_scale, x4_scales)
+        nc.scalar.activation(out=warm[:], in_=warm[:], func=GELU)
+        make_identity(nc, ident[:])
+        nc.gpsimd.dma_start(out=bias_rows[0:M_TILES, :], in_=b.rearrange("(m p) -> m p", p=P))
+        load_scales(nc.gpsimd, w4_scale, w4_scales)
+
+        load_w8(1)
+        for i in range(len(loads)):
+            load_x8(i)
+
+        def views(grp, c0, c1, raw, r0):
+            dst = grp[:, c0:c1, :].rearrange("p (c i) j -> p c j i", i=4)
+            src = raw[:, :, r0 : r0 + c1 - c0].rearrange("p j (c i) -> p c j i", i=4)
+            return dst, src
+
+        def group_w(engine, a, c0, c1):
+            dst, src = views(w8_grp[a], c0, c1, w8_raw[a], c0)
+            engine(out=dst, in_=src)
+
+        def group_x(engine, i, c0, c1):
+            a, t0, t1 = loads[i]
+            dst, src = views(x8_grp[a], c0, c1, x8_raw[i], c0 - t0)
+            engine(out=dst, in_=src)
+
+        def quant(code, scale, grp, c0, width):
+            nc.vector.quantize_mx(
+                out=code[:, c0 : c0 + width].bitcast(E4M3X4),
+                scales=scale[:, c0 : c0 + width],
+                in_=grp[:, c0 : c0 + width, :].rearrange("p c j -> p (c j)"),
+            )
+
+        V, S = nc.vector.tensor_copy, nc.scalar.copy
+
+        def do_w(a):
+            group_w(V, a, 0, 256)
+            group_w(S, a, 256, 512)
+            quant(w8_code[a], w8_scale[a], w8_grp[a], 0, 256)
+            quant(w8_code[a], w8_scale[a], w8_grp[a], 256, 256)
+
+        def quant_x(a, c0):
+            quant(x8_code[a], x8_scale[a], x8_grp[a], c0, PIECE)
+
+        bank_of = {}
+
+        def open_bank(m, j):
+            bank = psum.tile([P, T_TILE], F32, name="bank%d" % (m + 4 * (j % 2)))
+            bank_of[m, j] = bank
+
+        def fp4(m, j, a, start):
+            nc.tensor.matmul_mx(
+                out=bank_of[m, j][:],
+                lhsT=w4_word[:, a, 2 * P * m : 2 * P * (m + 1)].bitcast(E2M1X4),
+                lhsT_scale=w4_scale[:, a, P * m : P * (m + 1)],
+                rhs=x4_word[:, a, 2 * T_TILE * j : 2 * T_TILE * (j + 1)].bitcast(E2M1X4),
+                rhs_scale=x4_scale[:, a, T_TILE * j : T_TILE * (j + 1)],
+                start=start,
+                stop=False,
+            )
+
+        def fp8(m, j, a, stop):
+            nc.tensor.matmul_mx(
+                out=bank_of[m, j][:],
+                lhsT=w8_code[a][:, P * m : P * (m + 1)].bitcast(E4M3X4),
+                lhsT_scale=w8_scale[a][:, P * m : P * (m + 1)],
+                rhs=x8_code[a][:, T_TILE * j : T_TILE * (j + 1)].bitcast(E4M3X4),
+                rhs_scale=x8_scale[a][:, T_TILE * j : T_TILE * (j + 1)],
+                start=False,
+                stop=stop,
+            )
+
+        def finish(m, j):
+            res = results.tile([P, T_TILE], F32, name="res")
+            nc.scalar.activation(out=res[:], in_=bank_of[m, j][:], func=GELU, bias=bias[:, m : m + 1])
+            nc.sync.dma_start(out=out[P * m : P * (m + 1), T_TILE * j : T_TILE * (j + 1)], in_=res[:])
+
+        bias_bank = psum.tile([P, T_TILE], F32, name="bank7")
+        nc.tensor.transpose(bias_bank[:, 0:P], bias_rows[:], ident[:])
+
+        do_w(0)
+        nc.vector.tensor_copy(out=bias[:], in_=bias_bank[:, 0:M_TILES])
+        do_w(1)
+
+        for j in range(2):
+            for m in range(M_TILES):
+                open_bank(m, j)
+                fp4(m, j, 0, True)
+                fp4(m, j, 1, False)
+
+        for i in range(2):
+            t0 = 768 * i
+            group_x(S, i, t0 + 512, t0 + 768)
+            group_x(V, i, t0, t0 + 256)
+            group_x(V, i, t0 + 256, t0 + 512)
+            quant_x(0, t0)
+            quant_x(0, t0 + 256)
+            quant_x(0, t0 + 512)
+        for j in range(2):
+            for m in range(M_TILES):
+                fp8(m, j, 0, False)
+
+        group_x(S, 2, 320, 512)
+        group_x(V, 2, 0, 320)
+        quant_x(1, 0)
+        quant_x(1, 256)
+        for m in range(M_TILES):
+            fp8(m, 0, 1, True)
+        for m in range(M_TILES):
+            finish(m, 0)
+
+        group_x(V, 3, 512, 768)
+        group_x(V, 3, 768, 1024)
+        quant_x(1, 512)
+        quant_x(1, 768)
+
+        def open_last(m):
+            open_bank(m, 2)
+            fp4(m, 2, 0, True)
+            fp4(m, 2, 1, False)
+            fp8(m, 2, 0, False)
+
+        open_last(0)
+        open_last(1)
+        for m in range(M_TILES):
+            fp8(m, 1, 1, True)
+        for m in range(M_TILES):
+            finish(m, 1)
+        open_last(2)
+        open_last(3)
+
+        group_x(V, 4, 1024, 1280)
+        group_x(V, 4, 1280, 1536)
+        quant_x(1, 1024)
+        quant_x(1, 1280)
+        for m in range(M_TILES):
+            fp8(m, 2, 1, True)
+        for m in range(M_TILES):
+            finish(m, 2)

@@ -35,7 +35,7 @@ def tile_mix_atom_fm_gelu_kernel(tc, x8, w8, x4_words, x4_scales, w4_words, w4_s
         w8_grp = [keep.tile([P, N, 4], BF16, name="w8_grp%d" % a, align_bytes=64) for a in range(PASSES)]
         w8_code = [keep.tile([P, N], U32, name="w8_code%d" % a, align_bytes=64) for a in range(PASSES)]
         w8_scale = [keep.tile([P, N], U8, name="w8_scale%d" % a, align_bytes=64) for a in range(PASSES)]
-        loads = [(0, 0, 768), (0, 768, 1536), (1, 0, 512), (1, 512, 1024), (1, 1024, 1536)]
+        loads = [(0, 0, 1536), (1, 0, 512), (1, 512, 1024), (1, 1024, 1280), (1, 1280, 1536)]
         x8_raw = [keep.tile([P, 4, t1 - t0], F32, name="x8_raw%d_%d" % (a, t0), align_bytes=64) for a, t0, t1 in loads]
         x8_grp = [keep.tile([P, T, 4], BF16, name="x8_grp%d" % a, align_bytes=64) for a in range(PASSES)]
         x8_code = [keep.tile([P, T], U32, name="x8_code%d" % a, align_bytes=64) for a in range(PASSES)]
@@ -56,13 +56,12 @@ def tile_mix_atom_fm_gelu_kernel(tc, x8, w8, x4_words, x4_scales, w4_words, w4_s
             a, t0, t1 = loads[i]
             nc.sync.dma_start(out=x8_raw[i][:], in_=x8[512 * a : 512 * (a + 1), t0:t1].rearrange("(p j) t -> p j t", j=4))
 
-        load_w8(0)
         nc.sync.dma_start(out=w4_word[:].bitcast(I32), in_=w4_words.bitcast(I32).rearrange("a p w -> p a w"))
         nc.sync.dma_start(out=x4_word[:].bitcast(I32), in_=x4_words.bitcast(I32).rearrange("a p w -> p a w"))
 
         nc.vector.memset(x4_scale[:].bitcast(I32), 0)
-        nc.vector.memset(bias_rows[:], 0.0)
         nc.vector.memset(w4_scale[:].bitcast(I32), 0)
+        nc.vector.memset(bias_rows[:], 0.0)
         nc.vector.memset(warm[:], 0.0)
 
         def load_scales(engine, plane, source):
@@ -72,12 +71,14 @@ def tile_mix_atom_fm_gelu_kernel(tc, x8, w8, x4_words, x4_scales, w4_words, w4_s
 
         load_scales(nc.scalar, x4_scale, x4_scales)
         nc.scalar.activation(out=warm[:], in_=warm[:], func=GELU)
-        make_identity(nc, ident[:])
-        nc.gpsimd.dma_start(out=bias_rows[0:M_TILES, :], in_=b.rearrange("(m p) -> m p", p=P))
         load_scales(nc.gpsimd, w4_scale, w4_scales)
+        nc.gpsimd.dma_start(out=bias_rows[0:M_TILES, :], in_=b.rearrange("(m p) -> m p", p=P))
+        make_identity(nc, ident[:])
 
+        load_x8(0)
+        load_w8(0)
         load_w8(1)
-        for i in range(len(loads)):
+        for i in range(1, len(loads)):
             load_x8(i)
 
         def views(grp, c0, c1, raw, r0):
@@ -102,12 +103,6 @@ def tile_mix_atom_fm_gelu_kernel(tc, x8, w8, x4_words, x4_scales, w4_words, w4_s
             )
 
         V, S = nc.vector.tensor_copy, nc.scalar.copy
-
-        def do_w(a):
-            group_w(V, a, 0, 256)
-            group_w(S, a, 256, 512)
-            quant(w8_code[a], w8_scale[a], w8_grp[a], 0, 256)
-            quant(w8_code[a], w8_scale[a], w8_grp[a], 256, 256)
 
         def quant_x(a, c0):
             quant(x8_code[a], x8_scale[a], x8_grp[a], c0, PIECE)
@@ -145,33 +140,47 @@ def tile_mix_atom_fm_gelu_kernel(tc, x8, w8, x4_words, x4_scales, w4_words, w4_s
             nc.scalar.activation(out=res[:], in_=bank_of[m, j][:], func=GELU, bias=bias[:, m : m + 1])
             nc.sync.dma_start(out=out[P * m : P * (m + 1), T_TILE * j : T_TILE * (j + 1)], in_=res[:])
 
-        bias_bank = psum.tile([P, T_TILE], F32, name="bank7")
-        nc.tensor.transpose(bias_bank[:, 0:P], bias_rows[:], ident[:])
+        def open_fp4(m, j):
+            open_bank(m, j)
+            fp4(m, j, 0, True)
+            fp4(m, j, 1, False)
 
-        do_w(0)
-        nc.vector.tensor_copy(out=bias[:], in_=bias_bank[:, 0:M_TILES])
-        do_w(1)
+        def quant_w(a, c0):
+            quant(w8_code[a], w8_scale[a], w8_grp[a], c0, PIECE)
 
         for j in range(2):
             for m in range(M_TILES):
-                open_bank(m, j)
-                fp4(m, j, 0, True)
-                fp4(m, j, 1, False)
+                if (m, j) == (3, 1):
+                    bias_bank = psum.tile([P, T_TILE], F32, name="bank7")
+                    nc.tensor.transpose(bias_bank[:, 0:P], bias_rows[:], ident[:])
+                    nc.vector.tensor_copy(out=bias[:], in_=bias_bank[:, 0:M_TILES])
+                open_fp4(m, j)
 
-        for i in range(2):
-            t0 = 768 * i
-            group_x(S, i, t0 + 512, t0 + 768)
-            group_x(V, i, t0, t0 + 256)
-            group_x(V, i, t0 + 256, t0 + 512)
-            quant_x(0, t0)
-            quant_x(0, t0 + 256)
-            quant_x(0, t0 + 512)
+        for c0 in (256, 512, 768, 1280):
+            group_x(S, 0, c0, c0 + PIECE)
+        group_w(S, 1, 256, 512)
+
+        group_x(V, 0, 0, 256)
+        group_x(V, 0, 1024, 1280)
+        quant_x(0, 0)
+        quant_x(0, 256)
+        quant_x(0, 1024)
+        group_w(V, 0, 0, 256)
+        quant_x(0, 512)
+        quant_w(0, 0)
+        group_w(V, 0, 256, 512)
+        quant_x(0, 768)
+        quant_w(0, 256)
+        group_w(V, 1, 0, 256)
+        quant_x(0, 1280)
+        quant_w(1, 0)
         for j in range(2):
             for m in range(M_TILES):
                 fp8(m, j, 0, False)
 
-        group_x(S, 2, 320, 512)
-        group_x(V, 2, 0, 320)
+        group_x(S, 1, 256, 512)
+        group_x(V, 1, 0, 256)
+        quant_w(1, 256)
         quant_x(1, 0)
         quant_x(1, 256)
         for m in range(M_TILES):
@@ -179,31 +188,30 @@ def tile_mix_atom_fm_gelu_kernel(tc, x8, w8, x4_words, x4_scales, w4_words, w4_s
         for m in range(M_TILES):
             finish(m, 0)
 
-        group_x(V, 3, 512, 768)
-        group_x(V, 3, 768, 1024)
-        quant_x(1, 512)
-        quant_x(1, 768)
-
         def open_last(m):
-            open_bank(m, 2)
-            fp4(m, 2, 0, True)
-            fp4(m, 2, 1, False)
+            open_fp4(m, 2)
             fp8(m, 2, 0, False)
 
+        group_x(V, 2, 512, 768)
+        group_x(V, 2, 768, 1024)
+        quant_x(1, 512)
+        quant_x(1, 768)
         open_last(0)
         open_last(1)
         for m in range(M_TILES):
             fp8(m, 1, 1, True)
         for m in range(M_TILES):
             finish(m, 1)
-        open_last(2)
-        open_last(3)
 
-        group_x(V, 4, 1024, 1280)
+        group_x(V, 3, 1024, 1280)
         group_x(V, 4, 1280, 1536)
         quant_x(1, 1024)
         quant_x(1, 1280)
-        for m in range(M_TILES):
-            fp8(m, 2, 1, True)
+        open_last(2)
+        fp8(0, 2, 1, True)
+        fp8(1, 2, 1, True)
+        open_last(3)
+        fp8(2, 2, 1, True)
+        fp8(3, 2, 1, True)
         for m in range(M_TILES):
             finish(m, 2)

@@ -59,9 +59,9 @@ def tile_mix_atom_fm_gelu_kernel(tc, x8, w8, x4_words, x4_scales, w4_words, w4_s
         nc.sync.dma_start(out=w4_word[:].bitcast(I32), in_=w4_words.bitcast(I32).rearrange("a p w -> p a w"))
         nc.sync.dma_start(out=x4_word[:].bitcast(I32), in_=x4_words.bitcast(I32).rearrange("a p w -> p a w"))
 
-        nc.vector.memset(x4_scale[:].bitcast(I32), 0)
-        nc.vector.memset(w4_scale[:].bitcast(I32), 0)
         nc.vector.memset(bias_rows[:], 0.0)
+        nc.vector.memset(w4_scale[:].bitcast(I32), 0)
+        nc.vector.memset(x4_scale[:].bitcast(I32), 0)
         nc.vector.memset(warm[:], 0.0)
 
         def load_scales(engine, plane, source):
@@ -69,11 +69,11 @@ def tile_mix_atom_fm_gelu_kernel(tc, x8, w8, x4_words, x4_scales, w4_words, w4_s
             for r in range(4):
                 engine.dma_start(out=plane[:].bitcast(I32)[r:P:32], in_=rows[r])
 
+        make_identity(nc, ident[:])
+        nc.gpsimd.dma_start(out=bias_rows[0:M_TILES, :], in_=b.rearrange("(m p) -> m p", p=P))
+        load_scales(nc.sync, w4_scale, w4_scales)
         load_scales(nc.scalar, x4_scale, x4_scales)
         nc.scalar.activation(out=warm[:], in_=warm[:], func=GELU)
-        load_scales(nc.gpsimd, w4_scale, w4_scales)
-        nc.gpsimd.dma_start(out=bias_rows[0:M_TILES, :], in_=b.rearrange("(m p) -> m p", p=P))
-        make_identity(nc, ident[:])
 
         load_x8(0)
         load_w8(0)
@@ -148,12 +148,11 @@ def tile_mix_atom_fm_gelu_kernel(tc, x8, w8, x4_words, x4_scales, w4_words, w4_s
         def quant_w(a, c0):
             quant(w8_code[a], w8_scale[a], w8_grp[a], c0, PIECE)
 
+        bias_bank = psum.tile([P, T_TILE], F32, name="bank7")
+        nc.tensor.transpose(bias_bank[:, 0:P], bias_rows[:], ident[:])
+        nc.vector.tensor_copy(out=bias[:], in_=bias_bank[:, 0:M_TILES])
         for j in range(2):
             for m in range(M_TILES):
-                if (m, j) == (3, 1):
-                    bias_bank = psum.tile([P, T_TILE], F32, name="bank7")
-                    nc.tensor.transpose(bias_bank[:, 0:P], bias_rows[:], ident[:])
-                    nc.vector.tensor_copy(out=bias[:], in_=bias_bank[:, 0:M_TILES])
                 open_fp4(m, j)
 
         for c0 in (256, 512, 768, 1280):

@@ -35,13 +35,14 @@ def tile_mix_atom_fm_gelu_kernel(tc, x8, w8, x4_words, x4_scales, w4_words, w4_s
         w8_grp = [keep.tile([P, N, 4], BF16, name="w8_grp%d" % a, align_bytes=64) for a in range(PASSES)]
         w8_code = [keep.tile([P, N], U32, name="w8_code%d" % a, align_bytes=64) for a in range(PASSES)]
         w8_scale = [keep.tile([P, N], U8, name="w8_scale%d" % a, align_bytes=64) for a in range(PASSES)]
-        loads = [(0, 0, 1536), (1, 0, 512), (1, 512, 1024), (1, 1024, 1280), (1, 1280, 1536)]
+        loads = [(0, 0, 1024), (1, 0, 512), (0, 1024, 1536), (1, 512, 1024), (1, 1024, 1280), (1, 1280, 1536)]
         x8_raw = [keep.tile([P, 4, t1 - t0], F32, name="x8_raw%d_%d" % (a, t0), align_bytes=64) for a, t0, t1 in loads]
         x8_grp = [keep.tile([P, T, 4], BF16, name="x8_grp%d" % a, align_bytes=64) for a in range(PASSES)]
         x8_code = [keep.tile([P, T], U32, name="x8_code%d" % a, align_bytes=64) for a in range(PASSES)]
         x8_scale = [keep.tile([P, T], U8, name="x8_scale%d" % a, align_bytes=64) for a in range(PASSES)]
         w4_word = keep.tile([P, PASSES, 2 * N], U8, name="w4_word", align_bytes=64)
-        x4_word = keep.tile([P, PASSES, 2 * T], U8, name="x4_word", align_bytes=64)
+        x4_cuts = [(0, 1024), (1024, 1536)]
+        x4_word = [keep.tile([P, PASSES, 2 * (t1 - t0)], U8, name="x4_word%d" % t0, align_bytes=64) for t0, t1 in x4_cuts]
         w4_scale = keep.tile([P, PASSES, N], U8, name="w4_scale", align_bytes=64)
         x4_scale = keep.tile([P, PASSES, T], U8, name="x4_scale", align_bytes=64)
         ident = keep.tile([P, P], F32, name="ident", align_bytes=64)
@@ -57,7 +58,15 @@ def tile_mix_atom_fm_gelu_kernel(tc, x8, w8, x4_words, x4_scales, w4_words, w4_s
             nc.sync.dma_start(out=x8_raw[i][:], in_=x8[512 * a : 512 * (a + 1), t0:t1].rearrange("(p j) t -> p j t", j=4))
 
         nc.sync.dma_start(out=w4_word[:].bitcast(I32), in_=w4_words.bitcast(I32).rearrange("a p w -> p a w"))
-        nc.sync.dma_start(out=x4_word[:].bitcast(I32), in_=x4_words.bitcast(I32).rearrange("a p w -> p a w"))
+
+        def load_x4(i):
+            t0, t1 = x4_cuts[i]
+            nc.sync.dma_start(
+                out=x4_word[i][:].bitcast(I32),
+                in_=x4_words.bitcast(I32).rearrange("a p w -> p a w")[:, :, t0 // 2 : t1 // 2],
+            )
+
+        load_x4(0)
 
         nc.vector.memset(bias_rows[:], 0.0)
         nc.vector.memset(w4_scale[:].bitcast(I32), 0)
@@ -78,8 +87,12 @@ def tile_mix_atom_fm_gelu_kernel(tc, x8, w8, x4_words, x4_scales, w4_words, w4_s
         load_x8(0)
         load_w8(0)
         load_w8(1)
-        for i in range(1, len(loads)):
-            load_x8(i)
+        load_x8(1)
+        load_x8(2)
+        load_x8(3)
+        load_x4(1)
+        load_x8(4)
+        load_x8(5)
 
         def views(grp, c0, c1, raw, r0):
             dst = grp[:, c0:c1, :].rearrange("p (c i) j -> p c j i", i=4)
@@ -114,31 +127,35 @@ def tile_mix_atom_fm_gelu_kernel(tc, x8, w8, x4_words, x4_scales, w4_words, w4_s
             bank_of[m, j] = bank
 
         def fp4(m, j, a, start):
+            i, t0 = (0, T_TILE * j) if j < 2 else (1, 0)
             nc.tensor.matmul_mx(
                 out=bank_of[m, j][:],
                 lhsT=w4_word[:, a, 2 * P * m : 2 * P * (m + 1)].bitcast(E2M1X4),
                 lhsT_scale=w4_scale[:, a, P * m : P * (m + 1)],
-                rhs=x4_word[:, a, 2 * T_TILE * j : 2 * T_TILE * (j + 1)].bitcast(E2M1X4),
+                rhs=x4_word[i][:, a, 2 * t0 : 2 * (t0 + T_TILE)].bitcast(E2M1X4),
                 rhs_scale=x4_scale[:, a, T_TILE * j : T_TILE * (j + 1)],
                 start=start,
                 stop=False,
             )
 
-        def fp8(m, j, a, stop):
+        def fp8(m, j, a, start=False, stop=False):
             nc.tensor.matmul_mx(
                 out=bank_of[m, j][:],
                 lhsT=w8_code[a][:, P * m : P * (m + 1)].bitcast(E4M3X4),
                 lhsT_scale=w8_scale[a][:, P * m : P * (m + 1)],
                 rhs=x8_code[a][:, T_TILE * j : T_TILE * (j + 1)].bitcast(E4M3X4),
                 rhs_scale=x8_scale[a][:, T_TILE * j : T_TILE * (j + 1)],
-                start=False,
+                start=start,
                 stop=stop,
             )
 
-        def finish(m, j):
+        def finish(m, j, parts=1):
             res = results.tile([P, T_TILE], F32, name="res")
-            nc.scalar.activation(out=res[:], in_=bank_of[m, j][:], func=GELU, bias=bias[:, m : m + 1])
-            nc.sync.dma_start(out=out[P * m : P * (m + 1), T_TILE * j : T_TILE * (j + 1)], in_=res[:])
+            width = T_TILE // parts
+            for c0 in range(0, T_TILE, width):
+                cols = slice(c0, c0 + width)
+                nc.scalar.activation(out=res[:, cols], in_=bank_of[m, j][:, cols], func=GELU, bias=bias[:, m : m + 1])
+                nc.sync.dma_start(out=out[P * m : P * (m + 1), T_TILE * j + c0 : T_TILE * j + c0 + width], in_=res[:, cols])
 
         def open_fp4(m, j):
             open_bank(m, j)
@@ -155,62 +172,66 @@ def tile_mix_atom_fm_gelu_kernel(tc, x8, w8, x4_words, x4_scales, w4_words, w4_s
             for m in range(M_TILES):
                 open_fp4(m, j)
 
-        for c0 in (256, 512, 768, 1280):
-            group_x(S, 0, c0, c0 + PIECE)
+        group_x(S, 0, 256, 512)
+        group_x(S, 0, 512, 768)
+        group_w(S, 0, 0, 256)
+        group_w(S, 1, 0, 256)
         group_w(S, 1, 256, 512)
+        group_x(S, 1, 256, 512)
+        group_x(S, 2, 1024, 1280)
 
         group_x(V, 0, 0, 256)
-        group_x(V, 0, 1024, 1280)
+        group_x(V, 0, 768, 1024)
         quant_x(0, 0)
         quant_x(0, 256)
-        quant_x(0, 1024)
-        group_w(V, 0, 0, 256)
-        quant_x(0, 512)
-        quant_w(0, 0)
-        group_w(V, 0, 256, 512)
         quant_x(0, 768)
+        group_w(V, 0, 256, 512)
+        quant_x(0, 512)
         quant_w(0, 256)
-        group_w(V, 1, 0, 256)
-        quant_x(0, 1280)
+        quant_w(0, 0)
         quant_w(1, 0)
         for j in range(2):
             for m in range(M_TILES):
-                fp8(m, j, 0, False)
-
-        group_x(S, 1, 256, 512)
+                fp8(m, j, 0)
         group_x(V, 1, 0, 256)
         quant_w(1, 256)
         quant_x(1, 0)
+        group_x(V, 2, 1280, 1536)
         quant_x(1, 256)
         for m in range(M_TILES):
-            fp8(m, 0, 1, True)
+            fp8(m, 0, 1, stop=True)
         for m in range(M_TILES):
             finish(m, 0)
+        quant_x(0, 1280)
+        quant_x(0, 1024)
 
         def open_last(m):
-            open_fp4(m, 2)
-            fp8(m, 2, 0, False)
+            open_bank(m, 2)
+            fp8(m, 2, 0, start=True)
+            fp4(m, 2, 0, False)
+            fp4(m, 2, 1, False)
 
-        group_x(V, 2, 512, 768)
-        group_x(V, 2, 768, 1024)
+        group_x(V, 3, 512, 768)
+        group_x(V, 3, 768, 1024)
         quant_x(1, 512)
         quant_x(1, 768)
         open_last(0)
         open_last(1)
         for m in range(M_TILES):
-            fp8(m, 1, 1, True)
+            fp8(m, 1, 1, stop=True)
         for m in range(M_TILES):
             finish(m, 1)
 
-        group_x(V, 3, 1024, 1280)
-        group_x(V, 4, 1280, 1536)
+        group_x(V, 4, 1024, 1280)
+        group_x(V, 5, 1280, 1536)
         quant_x(1, 1024)
         quant_x(1, 1280)
         open_last(2)
-        fp8(0, 2, 1, True)
-        fp8(1, 2, 1, True)
+        fp8(0, 2, 1, stop=True)
+        fp8(1, 2, 1, stop=True)
         open_last(3)
-        fp8(2, 2, 1, True)
-        fp8(3, 2, 1, True)
-        for m in range(M_TILES):
+        fp8(2, 2, 1, stop=True)
+        fp8(3, 2, 1, stop=True)
+        for m in range(M_TILES - 1):
             finish(m, 2)
+        finish(M_TILES - 1, 2, parts=2)

from contextlib import ExitStack

import concourse.mybir as mybir
from concourse.masks import make_identity

K, N, T = 1024, 512, 1536

F32 = mybir.dt.float32
BF16 = mybir.dt.bfloat16
I32 = mybir.dt.int32
U32 = mybir.dt.uint32
U8 = mybir.dt.uint8
E4M3X4 = mybir.dt.float8_e4m3fn_x4
E2M1X4 = mybir.dt.float4_e2m1fn_x4
GELU = mybir.ActivationFunctionType.Gelu_apprx_tanh

P = 128
PASSES = 2
M_TILES = N // P
T_TILE = 512
PIECE = 256

FLOPS = 2 * N * (2 * K) * T


def tile_mix_atom_fm_gelu_kernel(tc, x8, w8, x4_words, x4_scales, w4_words, w4_scales, b, out):
    nc = tc.nc
    with ExitStack() as ctx:
        keep = ctx.enter_context(tc.tile_pool(name="keep", bufs=1))
        results = ctx.enter_context(tc.tile_pool(name="results", bufs=12))
        psum = ctx.enter_context(tc.psum_pool(name="psum", bufs=1))
        ctx.enter_context(tc.manual_schedule())

        w8_raw = [keep.tile([P, 4, N], F32, name="w8_raw%d" % a, align_bytes=64) for a in range(PASSES)]
        w8_grp = [keep.tile([P, N, 4], BF16, name="w8_grp%d" % a, align_bytes=64) for a in range(PASSES)]
        w8_code = [keep.tile([P, N], U32, name="w8_code%d" % a, align_bytes=64) for a in range(PASSES)]
        w8_scale = [keep.tile([P, N], U8, name="w8_scale%d" % a, align_bytes=64) for a in range(PASSES)]
        loads = [(0, 0, 1024), (1, 0, 512), (0, 1024, 1536), (1, 512, 1024), (1, 1024, 1280), (1, 1280, 1536)]
        x8_raw = [keep.tile([P, 4, t1 - t0], F32, name="x8_raw%d_%d" % (a, t0), align_bytes=64) for a, t0, t1 in loads]
        x8_grp = [keep.tile([P, T, 4], BF16, name="x8_grp%d" % a, align_bytes=64) for a in range(PASSES)]
        x8_code = [keep.tile([P, T], U32, name="x8_code%d" % a, align_bytes=64) for a in range(PASSES)]
        x8_scale = [keep.tile([P, T], U8, name="x8_scale%d" % a, align_bytes=64) for a in range(PASSES)]
        w4_word = keep.tile([P, PASSES, 2 * N], U8, name="w4_word", align_bytes=64)
        x4_cuts = [(0, 1024), (1024, 1536)]
        x4_word = [keep.tile([P, PASSES, 2 * (t1 - t0)], U8, name="x4_word%d" % t0, align_bytes=64) for t0, t1 in x4_cuts]
        w4_scale = keep.tile([P, PASSES, N], U8, name="w4_scale", align_bytes=64)
        x4_scale = keep.tile([P, PASSES, T], U8, name="x4_scale", align_bytes=64)
        ident = keep.tile([P, P], F32, name="ident", align_bytes=64)
        bias_rows = keep.tile([P, P], F32, name="bias_rows", align_bytes=64)
        bias = keep.tile([P, M_TILES], F32, name="bias", align_bytes=64)
        warm = keep.tile([P, 1], F32, name="warm", align_bytes=64)

        def load_w8(a):
            nc.sync.dma_start(out=w8_raw[a][:], in_=w8[512 * a : 512 * (a + 1), :].rearrange("(p j) n -> p j n", j=4))

        def load_x8(i):
            a, t0, t1 = loads[i]
            nc.sync.dma_start(out=x8_raw[i][:], in_=x8[512 * a : 512 * (a + 1), t0:t1].rearrange("(p j) t -> p j t", j=4))

        nc.sync.dma_start(out=w4_word[:].bitcast(I32), in_=w4_words.bitcast(I32).rearrange("a p w -> p a w"))

        def load_x4(i):
            t0, t1 = x4_cuts[i]
            nc.sync.dma_start(
                out=x4_word[i][:].bitcast(I32),
                in_=x4_words.bitcast(I32).rearrange("a p w -> p a w")[:, :, t0 // 2 : t1 // 2],
            )

        load_x4(0)

        nc.vector.memset(bias_rows[:], 0.0)
        nc.vector.memset(w4_scale[:].bitcast(I32), 0)
        nc.vector.memset(x4_scale[:].bitcast(I32), 0)
        nc.vector.memset(warm[:], 0.0)

        def load_scales(engine, plane, source):
            rows = source.bitcast(I32).rearrange("a (q r) c -> r q a c", r=4)
            for r in range(4):
                engine.dma_start(out=plane[:].bitcast(I32)[r:P:32], in_=rows[r])

        make_identity(nc, ident[:])
        nc.gpsimd.dma_start(out=bias_rows[0:M_TILES, :], in_=b.rearrange("(m p) -> m p", p=P))
        load_scales(nc.sync, w4_scale, w4_scales)
        load_scales(nc.scalar, x4_scale, x4_scales)
        nc.scalar.activation(out=warm[:], in_=warm[:], func=GELU)

        load_x8(0)
        load_w8(0)
        load_w8(1)
        load_x8(1)
        load_x8(2)
        load_x8(3)
        load_x4(1)
        load_x8(4)
        load_x8(5)

        def views(grp, c0, c1, raw, r0):
            dst = grp[:, c0:c1, :].rearrange("p (c i) j -> p c j i", i=4)
            src = raw[:, :, r0 : r0 + c1 - c0].rearrange("p j (c i) -> p c j i", i=4)
            return dst, src

        def group_w(engine, a, c0, c1):
            dst, src = views(w8_grp[a], c0, c1, w8_raw[a], c0)
            engine(out=dst, in_=src)

        def group_x(engine, i, c0, c1):
            a, t0, t1 = loads[i]
            dst, src = views(x8_grp[a], c0, c1, x8_raw[i], c0 - t0)
            engine(out=dst, in_=src)

        def quant(code, scale, grp, c0, width):
            nc.vector.quantize_mx(
                out=code[:, c0 : c0 + width].bitcast(E4M3X4),
                scales=scale[:, c0 : c0 + width],
                in_=grp[:, c0 : c0 + width, :].rearrange("p c j -> p (c j)"),
            )

        V, S = nc.vector.tensor_copy, nc.scalar.copy

        def quant_x(a, c0):
            quant(x8_code[a], x8_scale[a], x8_grp[a], c0, PIECE)

        bank_of = {}

        def open_bank(m, j):
            bank = psum.tile([P, T_TILE], F32, name="bank%d" % (m + 4 * (j % 2)))
            bank_of[m, j] = bank

        def fp4(m, j, a, start):
            i, t0 = (0, T_TILE * j) if j < 2 else (1, 0)
            nc.tensor.matmul_mx(
                out=bank_of[m, j][:],
                lhsT=w4_word[:, a, 2 * P * m : 2 * P * (m + 1)].bitcast(E2M1X4),
                lhsT_scale=w4_scale[:, a, P * m : P * (m + 1)],
                rhs=x4_word[i][:, a, 2 * t0 : 2 * (t0 + T_TILE)].bitcast(E2M1X4),
                rhs_scale=x4_scale[:, a, T_TILE * j : T_TILE * (j + 1)],
                start=start,
                stop=False,
            )

        def fp8(m, j, a, start=False, stop=False):
            nc.tensor.matmul_mx(
                out=bank_of[m, j][:],
                lhsT=w8_code[a][:, P * m : P * (m + 1)].bitcast(E4M3X4),
                lhsT_scale=w8_scale[a][:, P * m : P * (m + 1)],
                rhs=x8_code[a][:, T_TILE * j : T_TILE * (j + 1)].bitcast(E4M3X4),
                rhs_scale=x8_scale[a][:, T_TILE * j : T_TILE * (j + 1)],
                start=start,
                stop=stop,
            )

        def finish(m, j, parts=1):
            res = results.tile([P, T_TILE], F32, name="res")
            width = T_TILE // parts
            for c0 in range(0, T_TILE, width):
                cols = slice(c0, c0 + width)
                nc.scalar.activation(out=res[:, cols], in_=bank_of[m, j][:, cols], func=GELU, bias=bias[:, m : m + 1])
                nc.sync.dma_start(out=out[P * m : P * (m + 1), T_TILE * j + c0 : T_TILE * j + c0 + width], in_=res[:, cols])

        def open_fp4(m, j):
            open_bank(m, j)
            fp4(m, j, 0, True)
            fp4(m, j, 1, False)

        def quant_w(a, c0):
            quant(w8_code[a], w8_scale[a], w8_grp[a], c0, PIECE)

        bias_bank = psum.tile([P, T_TILE], F32, name="bank7")
        nc.tensor.transpose(bias_bank[:, 0:P], bias_rows[:], ident[:])
        nc.vector.tensor_copy(out=bias[:], in_=bias_bank[:, 0:M_TILES])
        for j in range(2):
            for m in range(M_TILES):
                open_fp4(m, j)

        group_x(S, 0, 256, 512)
        group_x(S, 0, 512, 768)
        group_w(S, 0, 0, 256)
        group_w(S, 1, 0, 256)
        group_w(S, 1, 256, 512)
        group_x(S, 1, 256, 512)
        group_x(S, 2, 1024, 1280)

        group_x(V, 0, 0, 256)
        group_x(V, 0, 768, 1024)
        quant_x(0, 0)
        quant_x(0, 256)
        quant_x(0, 768)
        group_w(V, 0, 256, 512)
        quant_x(0, 512)
        quant_w(0, 256)
        quant_w(0, 0)
        quant_w(1, 0)
        for j in range(2):
            for m in range(M_TILES):
                fp8(m, j, 0)
        group_x(V, 1, 0, 256)
        quant_w(1, 256)
        quant_x(1, 0)
        group_x(V, 2, 1280, 1536)
        quant_x(1, 256)
        for m in range(M_TILES):
            fp8(m, 0, 1, stop=True)
        for m in range(M_TILES):
            finish(m, 0)
        quant_x(0, 1280)
        quant_x(0, 1024)

        def open_last(m):
            open_bank(m, 2)
            fp8(m, 2, 0, start=True)
            fp4(m, 2, 0, False)
            fp4(m, 2, 1, False)

        group_x(V, 3, 512, 768)
        group_x(V, 3, 768, 1024)
        quant_x(1, 512)
        quant_x(1, 768)
        open_last(0)
        open_last(1)
        for m in range(M_TILES):
            fp8(m, 1, 1, stop=True)
        for m in range(M_TILES):
            finish(m, 1)

        group_x(V, 4, 1024, 1280)
        group_x(V, 5, 1280, 1536)
        quant_x(1, 1024)
        quant_x(1, 1280)
        open_last(2)
        fp8(0, 2, 1, stop=True)
        fp8(1, 2, 1, stop=True)
        open_last(3)
        fp8(2, 2, 1, stop=True)
        fp8(3, 2, 1, stop=True)
        for m in range(M_TILES - 1):
            finish(m, 2)
        finish(M_TILES - 1, 2, parts=2)
